import numpy as np
import ml_dtypes


def mxq(x, axis, fmt="e4m3"):
    dtype, down = {"e4m3": (ml_dtypes.float8_e4m3fn, 7), "e5m2": (ml_dtypes.float8_e5m2, 14)}[fmt]
    v = np.moveaxis(np.asarray(x, np.float32).astype(ml_dtypes.bfloat16).astype(np.float64), axis, -1)
    blocks = v.reshape(v.shape[:-1] + (-1, 32))
    amax = np.abs(blocks).max(-1, keepdims=True)
    byte = np.maximum(np.where(amax > 0, np.frexp(amax)[1] - 1 + 127, 0) - down, 1)
    scale = np.exp2(byte - 127.0)
    codes = (blocks / scale).astype(np.float32).astype(dtype).astype(np.float64)
    return np.moveaxis((codes * scale).reshape(v.shape), -1, axis)


WIDE = False


def mx_kscale(k):
    if not WIDE:
        return np.ones(k)
    levels = np.array([10, -10, 5, -5, 0])
    if k % 512:
        return np.exp2(np.random.permutation(np.resize(levels, k // 32))).repeat(32)
    a = np.empty((k // 512, 16))
    for p in range(k // 512):
        a[p, :8] = np.random.permutation(np.resize(levels, 8))
        for g in range(8):
            far = levels[np.abs(levels - a[p, g]) >= 10]
            a[p, g + 8] = far[np.random.randint(len(far))]
    return np.exp2(a.ravel()).repeat(32)


def f64(x):
    return np.asarray(x).astype(np.float64)


def striped(idx):
    return np.tile(np.asarray(idx).reshape(-1, 16).T, (8, 1)).astype(np.uint16)


def unstriped(offs):
    return offs[:16].T.reshape(-1).astype(np.int64)


E2M1 = np.array([0.0, 0.5, 1.0, 1.5, 2.0, 3.0, 4.0, 6.0, -0.0, -0.5, -1.0, -1.5, -2.0, -3.0, -4.0, -6.0])


def pack_weight(w, fmt):
    k, n = w.shape
    w = f64(np.asarray(w, np.float32).astype(ml_dtypes.bfloat16)).reshape(k // 32, 32, n)
    amax = np.abs(w).max(1)
    if fmt == "e4m3":
        byte = np.frexp(amax)[1] - 1 + 127 - 7
    else:
        mant, ex = np.frexp(amax / 6.0)
        byte = np.where(mant > 0.5, ex, ex - 1) + 127
    byte = np.clip(np.where(amax > 0, byte, 1), 1, 254)
    scaled = (w * np.exp2(127.0 - byte)[:, None, :]).reshape(k, n).astype(np.float32)
    by_word = np.ascontiguousarray(scaled.reshape(k // 512, 128, 4, n).transpose(0, 1, 3, 2))
    if fmt == "e4m3":
        words = by_word.astype(ml_dtypes.float8_e4m3fn).view(np.uint8)
    else:
        c = by_word.astype(ml_dtypes.float4_e2m1fn).view(np.uint8) & 0xF
        words = (c[..., 0::2] | (c[..., 1::2] << 4)).reshape(k // 512, 128, 2 * n)
    return np.ascontiguousarray(words), np.ascontiguousarray(byte.astype(np.uint8).reshape(k // 512, 16, n))


def unpack_weight(words, scales, fmt):
    g, _, n = scales.shape
    words = np.ascontiguousarray(words).reshape(g, 128, n, -1)
    if fmt == "e4m3":
        vals = words.view(ml_dtypes.float8_e4m3fn).astype(np.float64)
    else:
        nib = np.empty((g, 128, n, 4), np.uint8)
        nib[..., 0::2] = words & 0xF
        nib[..., 1::2] = words >> 4
        vals = E2M1[nib]
    vals = vals * np.repeat(np.exp2(scales.astype(np.float64) - 127.0), 8, axis=1)[..., None]
    return vals.transpose(0, 1, 3, 2).reshape(g * 512, n)


def sigmoid(v):
    return 1.0 / (1.0 + np.exp(-v))


K, R, F, T, J = 512, 128, 512, 2048, 512


def setup_inputs():
    n = np.random.standard_normal
    idx = np.random.permutation(T)[:J]
    idx2 = np.random.permutation(T)[:J]
    fk = mx_kscale(K)
    tabp = pack_weight(n((K, T)) / fk[:, None], "e4m3")
    dtabp = pack_weight(n((K, T)) / fk[:, None], "e4m3")
    tab2p = pack_weight(n((K, T)) / fk[:, None], "e4m3")
    dtab2p = pack_weight(n((K, T)) / fk[:, None], "e4m3")
    return {
        "tab_words": tabp[0],
        "tab_scales": tabp[1],
        "dtab_words": dtabp[0],
        "dtab_scales": dtabp[1],
        "w1": (n((K, R)) * 1 / np.sqrt(K) * fk[:, None]).astype(np.float32),
        "tab2_words": tab2p[0],
        "tab2_scales": tab2p[1],
        "dtab2_words": dtab2p[0],
        "dtab2_scales": dtab2p[1],
        "w2": (n((K, R)) * 1 / np.sqrt(K) * fk[:, None]).astype(np.float32),
        "bias": (np.random.uniform(-0.5, 0.5, (R, 1))).astype(np.float32),
        "og": (np.random.uniform(0.5, 2.0, (R, 1))).astype(np.float32),
        "base": (0.3 * n((R, J))).astype(np.float32),
        "offs": striped(idx),
        "offs2": striped(idx2),
    }


def reference(tab_words, tab_scales, dtab_words, dtab_scales, w1, tab2_words, tab2_scales, dtab2_words, dtab2_scales, w2, bias, og, base, offs, offs2):
    idx = unstriped(offs)
    idx2 = unstriped(offs2)
    tabu = unpack_weight(tab_words, tab_scales, "e4m3")
    dtabu = unpack_weight(dtab_words, dtab_scales, "e4m3")
    tab2u = unpack_weight(tab2_words, tab2_scales, "e4m3")
    dtab2u = unpack_weight(dtab2_words, dtab2_scales, "e4m3")
    w1q = mxq(f64(w1), 0, "e4m3")
    tabidxg = tabu[:, idx]
    a = w1q.T @ tabidxg
    dtabidxg = dtabu[:, idx]
    ta = w1q.T @ dtabidxg
    w2q = mxq(f64(w2), 0, "e4m3")
    tab2idx2g = tab2u[:, idx2]
    b = w2q.T @ tab2idx2g
    dtab2idx2g = dtab2u[:, idx2]
    tb = w2q.T @ dtab2idx2g
    h1 = np.tanh(a)
    gt = sigmoid(b + f64(bias))
    th1 = ta * (1.0 - np.square(h1))
    tgt = tb * gt * (1.0 - gt)
    tu1 = th1 * gt + tgt * h1
    y = tu1 * f64(og) + f64(base)
    return y

@@ -1,0 +1,142 @@
+from contextlib import ExitStack
+
+import concourse.mybir as mybir
+
+F32 = mybir.dt.float32
+BF16 = mybir.dt.bfloat16
+I32 = mybir.dt.int32
+U32 = mybir.dt.uint32
+U16 = mybir.dt.uint16
+U8 = mybir.dt.uint8
+FP8X4 = mybir.dt.float8_e4m3fn_x4
+ALU = mybir.AluOpType
+ACT = mybir.ActivationFunctionType
+
+P = 128
+K, R, T, J = 512, 128, 2048, 512
+FLOPS = 4 * 2 * K * R * J
+HALF = J // 2
+ROW0 = P - 16
+
+
+def tile_attend_tctwotables_kernel(tc, tab_words, tab_scales, dtab_words, dtab_scales, w1,
+                                    tab2_words, tab2_scales, dtab2_words, dtab2_scales, w2,
+                                    bias, og, base, offs, offs2, out):
+    nc = tc.nc
+    with ExitStack() as ctx:
+        keep = ctx.enter_context(tc.tile_pool(name="keep", bufs=1))
+        psum = ctx.enter_context(tc.psum_pool(name="psum", bufs=1))
+
+        def load_list(name, src):
+            t = keep.tile([P, J // 16], U16, name=name)
+            nc.sync.dma_start(t[:], src)
+            return t
+
+        def load_words(name, src, q, tag):
+            t = keep.tile([P, T], U32, name=name, tag=tag)
+            q.dma_start(t[:].bitcast(I32), src[0].rearrange("p n t -> p (n t)").bitcast(I32))
+            return t
+
+        def load_scales(name, src, q, eng):
+            t = keep.tile([P, T], U8, name=name, tag=name)
+            q.dma_start(t[ROW0:P, :].bitcast(I32), src[0].bitcast(I32))
+            eng.memset(t[0:ROW0, :].bitcast(I32), 0)
+            return t
+
+        def gather_planes(name, windows, lists, q, eng):
+            rows = keep.tile([P, 2 * J], U8, name=name + "_rows")
+            plane = keep.tile([P, 2 * J], U8, name=name + "_plane", align_bytes=64)
+            eng.memset(plane[:].bitcast(I32), 0)
+            for i in range(2):
+                nc.vector.tensor_copy(rows[:, i * J:(i + 1) * J], windows[i][:].indirect(lists[i][:]))
+            for quad in range(4):
+                q.dma_start(plane[32 * quad: 32 * quad + 4, :].bitcast(I32),
+                            rows[ROW0 + 4 * quad: ROW0 + 4 * quad + 4, :].bitcast(I32))
+            return plane
+
+        def load_weight(name, src, q, tag):
+            t = keep.tile([P, 4, R], F32, name=name, tag=tag)
+            q.dma_start(t[:], src.rearrange("(p j) r -> p j r", j=4))
+            return t
+
+        def quantise(name, raw):
+            woven = keep.tile([P, R, 4], BF16, name=name + "_bf", align_bytes=64)
+            nc.scalar.copy(woven[:], raw[:].rearrange("p j r -> p r j"))
+            codes = keep.tile([P, R], U32, name=name + "_codes", align_bytes=64)
+            scales = keep.tile([P, R], U8, name=name + "_scales", align_bytes=64)
+            nc.vector.quantize_mx(codes[:].bitcast(FP8X4), scales[:], woven[:].rearrange("p r j -> p (r j)"))
+            return codes, scales
+
+        def gather(name, window, offsets, dtype, n):
+            g = keep.tile([P, n], dtype, name=name, align_bytes=64)
+            nc.vector.tensor_copy(g[:], window[:].indirect(offsets))
+            return g
+
+        def product(name, wq, words, plane, n):
+            acc = psum.tile([P, n], F32, name=name)
+            nc.tensor.matmul_mx(acc[:], lhsT=wq[0][:].bitcast(FP8X4), lhsT_scale=wq[1][:],
+                                rhs=words.bitcast(FP8X4), rhs_scale=plane, start=True, stop=True)
+            return acc
+
+        sy, ac, gp, ve = nc.sync, nc.scalar, nc.gpsimd, nc.vector
+        list2 = load_list("list2", offs2)
+        s2 = load_scales("s2", tab2_scales, sy, ve)
+        list1 = load_list("list1", offs)
+        s1 = load_scales("s1", tab_scales, sy, ve)
+        sd2 = load_scales("sd2", dtab2_scales, sy, ve)
+        sd1 = load_scales("sd1", dtab_scales, sy, ve)
+        x2 = load_words("x2", tab2_words, sy, "A")
+        w2_raw = load_weight("w2_raw", w2, sy, "B")
+        x1 = load_words("x1", tab_words, sy, "C")
+        w1_raw = load_weight("w1_raw", w1, sy, "D")
+        bias_c = keep.tile([P, 1], F32, name="bias_c")
+        og_c = keep.tile([P, 1], F32, name="og_c")
+        gp.dma_start(bias_c[:], bias)
+        gp.dma_start(og_c[:], og)
+
+        plane = gather_planes("fwd", (s2, s1), (list2, list1), sy, ve)
+        xd2 = load_words("xd2", dtab2_words, sy, "s1")
+        dplane = gather_planes("tan", (sd2, sd1), (list2, list1), sy, ve)
+        xd1 = load_words("xd1", dtab_words, sy, "sd1")
+
+        gx2 = gather("gx2", x2, list2[:], U32, J)
+        w2q = quantise("w2", w2_raw)
+        b = product("b", w2q, gx2[:], plane[:, 0:J], J)
+        g = keep.tile([P, J], F32, name="g")
+        nc.scalar.activation(g[:], b[:], ACT.Sigmoid, bias=bias_c[:])
+        gq = keep.tile([P, J], F32, name="gq")
+        nc.scalar.activation(gq[:], g[:], ACT.Square, bias=-0.5)
+
+        gx1 = gather("gx1", x1, list1[:], U32, J)
+        w1q = quantise("w1", w1_raw)
+        base_sb = keep.tile([P, J], F32, name="base_sb", tag="D")
+        sy.dma_start(base_sb[:], base)
+        a = product("a", w1q, gx1[:], plane[:, J:2 * J], J)
+        h = keep.tile([P, J], F32, name="h")
+        nc.scalar.activation(h[:], a[:], ACT.Tanh)
+        hq = keep.tile([P, J], F32, name="hq")
+        nc.scalar.activation(hq[:], h[:], ACT.Square)
+
+        gxd2 = gather("gxd2", xd2, list2[:], U32, J)
+        tb = product("tb", w2q, gxd2[:], dplane[:, 0:J], J)
+
+        fb = keep.tile([P, J], F32, name="fb")
+        nc.vector.scalar_tensor_tensor(fb[:], gq[:], 0.25, h[:], ALU.subtract, ALU.mult)
+        fa = keep.tile([P, J], F32, name="fa")
+        nc.vector.scalar_tensor_tensor(fa[:], hq[:], 1.0, g[:], ALU.subtract, ALU.mult)
+        tb_term = keep.tile([P, J], F32, name="tb_term")
+        nc.vector.scalar_tensor_tensor(tb_term[:], tb[:], og_c[:], fb[:], ALU.mult, ALU.mult)
+        part = keep.tile([P, J], F32, name="part")
+        nc.vector.tensor_tensor(part[:], base_sb[:], tb_term[:], ALU.subtract)
+
+        halves = []
+        for i in range(2):
+            gx = gather("gxd1_%d" % i, xd1, list1[:, i * 16:(i + 1) * 16], U32, HALF)
+            halves.append(product("ta%d" % i, w1q, gx[:], dplane[:, J + i * HALF:J + (i + 1) * HALF], HALF))
+        for i in range(2):
+            cols = slice(i * HALF, (i + 1) * HALF)
+            ta_term = keep.tile([P, HALF], F32, name="ta_term%d" % i)
+            nc.vector.scalar_tensor_tensor(ta_term[:], halves[i][:], og_c[:], fa[:, cols], ALU.mult, ALU.mult)
+            res = keep.tile([P, HALF], F32, name="res%d" % i)
+            nc.vector.tensor_tensor(res[:], part[:, cols], ta_term[:], ALU.subtract)
+            nc.sync.dma_start(out[:, cols], res[:])

@@ -43,12 +43,12 @@ def tile_attend_tctwotables_kernel(tc, tab_words, tab_scales, dtab_words, dtab_s
             eng.memset(t[0:ROW0, :].bitcast(I32), 0)
             return t
 
-        def gather_planes(name, windows, lists, q, eng):
-            rows = keep.tile([P, 2 * J], U8, name=name + "_rows")
-            plane = keep.tile([P, 2 * J], U8, name=name + "_plane", align_bytes=64)
-            eng.memset(plane[:].bitcast(I32), 0)
-            for i in range(2):
-                nc.vector.tensor_copy(rows[:, i * J:(i + 1) * J], windows[i][:].indirect(lists[i][:]))
+        def gather_rows(rows, i, window, offsets):
+            nc.vector.tensor_copy(rows[:, i * J:(i + 1) * J], window[:].indirect(offsets[:]))
+
+        def spread_rows(name, rows, q):
+            plane = keep.tile([P, 2 * J], U8, name=name, align_bytes=64)
+            nc.vector.memset(plane[:].bitcast(I32), 0)
             for quad in range(4):
                 q.dma_start(plane[32 * quad: 32 * quad + 4, :].bitcast(I32),
                             rows[ROW0 + 4 * quad: ROW0 + 4 * quad + 4, :].bitcast(I32))
@@ -84,48 +84,58 @@ def tile_attend_tctwotables_kernel(tc, tab_words, tab_scales, dtab_words, dtab_s
         list1 = load_list("list1", offs)
         s1 = load_scales("s1", tab_scales, sy, ve)
         sd2 = load_scales("sd2", dtab2_scales, sy, ve)
-        sd1 = load_scales("sd1", dtab_scales, sy, ve)
         x2 = load_words("x2", tab2_words, sy, "A")
         w2_raw = load_weight("w2_raw", w2, sy, "B")
         x1 = load_words("x1", tab_words, sy, "C")
-        w1_raw = load_weight("w1_raw", w1, sy, "D")
+        sd1 = load_scales("sd1", dtab_scales, sy, ve)
         bias_c = keep.tile([P, 1], F32, name="bias_c")
         og_c = keep.tile([P, 1], F32, name="og_c")
-        gp.dma_start(bias_c[:], bias)
-        gp.dma_start(og_c[:], og)
+        ac.dma_start(bias_c[:], bias)
+        ac.dma_start(og_c[:], og)
 
-        plane = gather_planes("fwd", (s2, s1), (list2, list1), sy, ve)
-        xd2 = load_words("xd2", dtab2_words, sy, "s1")
-        dplane = gather_planes("tan", (sd2, sd1), (list2, list1), sy, ve)
-        xd1 = load_words("xd1", dtab_words, sy, "sd1")
+        rows = keep.tile([P, 2 * J], U8, name="rows")
+        gather_rows(rows, 0, s2, list2)
+        gather_rows(rows, 1, s1, list1)
+        plane = spread_rows("plane", rows, sy)
+        w1_raw = load_weight("w1_raw", w1, sy, "s1")
+        drows = keep.tile([P, 2 * J], U8, name="drows")
+        gather_rows(drows, 0, sd2, list2)
+        xd2 = load_words("xd2", dtab2_words, sy, "sd2")
 
         gx2 = gather("gx2", x2, list2[:], U32, J)
         w2q = quantise("w2", w2_raw)
+        xd1 = load_words("xd1", dtab_words, sy, "A")
+        base_sb = keep.tile([P, J], F32, name="base_sb", tag="B")
+        sy.dma_start(base_sb[:], base)
         b = product("b", w2q, gx2[:], plane[:, 0:J], J)
-        g = keep.tile([P, J], F32, name="g")
-        nc.scalar.activation(g[:], b[:], ACT.Sigmoid, bias=bias_c[:])
+        half_bias = keep.tile([P, 1], F32, name="half_bias")
+        nc.scalar.mul(half_bias[:], bias_c[:], 0.5)
+        tau = keep.tile([P, J], F32, name="tau")
+        nc.scalar.activation(tau[:], b[:], ACT.Tanh, bias=half_bias[:], scale=0.5)
         gq = keep.tile([P, J], F32, name="gq")
-        nc.scalar.activation(gq[:], g[:], ACT.Square, bias=-0.5)
+        nc.scalar.activation(gq[:], tau[:], ACT.Square, scale=0.5)
 
         gx1 = gather("gx1", x1, list1[:], U32, J)
         w1q = quantise("w1", w1_raw)
-        base_sb = keep.tile([P, J], F32, name="base_sb", tag="D")
-        sy.dma_start(base_sb[:], base)
+        gather_rows(drows, 1, sd1, list1)
+        dplane = spread_rows("dplane", drows, sy)
         a = product("a", w1q, gx1[:], plane[:, J:2 * J], J)
         h = keep.tile([P, J], F32, name="h")
         nc.scalar.activation(h[:], a[:], ACT.Tanh)
         hq = keep.tile([P, J], F32, name="hq")
         nc.scalar.activation(hq[:], h[:], ACT.Square)
+        g = keep.tile([P, J], F32, name="g")
+        nc.scalar.activation(g[:], tau[:], ACT.Identity, bias=0.5, scale=0.5)
 
         gxd2 = gather("gxd2", xd2, list2[:], U32, J)
         tb = product("tb", w2q, gxd2[:], dplane[:, 0:J], J)
 
-        fb = keep.tile([P, J], F32, name="fb")
-        nc.vector.scalar_tensor_tensor(fb[:], gq[:], 0.25, h[:], ALU.subtract, ALU.mult)
-        fa = keep.tile([P, J], F32, name="fa")
-        nc.vector.scalar_tensor_tensor(fa[:], hq[:], 1.0, g[:], ALU.subtract, ALU.mult)
+        factors = keep.tile([P, 2 * J], F32, name="factors", tag="sd2")
+        fb, fa = factors[:, 0:J], factors[:, J:2 * J]
+        nc.vector.scalar_tensor_tensor(fb, gq[:], 0.25, h[:], ALU.subtract, ALU.mult)
+        nc.vector.scalar_tensor_tensor(fa, hq[:], 1.0, g[:], ALU.subtract, ALU.mult)
         tb_term = keep.tile([P, J], F32, name="tb_term")
-        nc.vector.scalar_tensor_tensor(tb_term[:], tb[:], og_c[:], fb[:], ALU.mult, ALU.mult)
+        nc.vector.scalar_tensor_tensor(tb_term[:], tb[:], og_c[:], fb, ALU.mult, ALU.mult)
         part = keep.tile([P, J], F32, name="part")
         nc.vector.tensor_tensor(part[:], base_sb[:], tb_term[:], ALU.subtract)
 
@@ -136,7 +146,7 @@ def tile_attend_tctwotables_kernel(tc, tab_words, tab_scales, dtab_words, dtab_s
         for i in range(2):
             cols = slice(i * HALF, (i + 1) * HALF)
             ta_term = keep.tile([P, HALF], F32, name="ta_term%d" % i)
-            nc.vector.scalar_tensor_tensor(ta_term[:], halves[i][:], og_c[:], fa[:, cols], ALU.mult, ALU.mult)
+            nc.vector.scalar_tensor_tensor(ta_term[:], halves[i][:], og_c[:], factors[:, J + i * HALF:J + (i + 1) * HALF], ALU.mult, ALU.mult)
             res = keep.tile([P, HALF], F32, name="res%d" % i)
             nc.vector.tensor_tensor(res[:], part[:, cols], ta_term[:], ALU.subtract)
             nc.sync.dma_start(out[:, cols], res[:])

@@ -48,7 +48,6 @@ def tile_attend_tctwotables_kernel(tc, tab_words, tab_scales, dtab_words, dtab_s
 
         def spread_rows(name, rows, q):
             plane = keep.tile([P, 2 * J], U8, name=name, align_bytes=64)
-            nc.vector.memset(plane[:].bitcast(I32), 0)
             for quad in range(4):
                 q.dma_start(plane[32 * quad: 32 * quad + 4, :].bitcast(I32),
                             rows[ROW0 + 4 * quad: ROW0 + 4 * quad + 4, :].bitcast(I32))
@@ -72,8 +71,8 @@ def tile_attend_tctwotables_kernel(tc, tab_words, tab_scales, dtab_words, dtab_s
             nc.vector.tensor_copy(g[:], window[:].indirect(offsets))
             return g
 
-        def product(name, wq, words, plane, n):
-            acc = psum.tile([P, n], F32, name=name)
+        def product(name, wq, words, plane, n, tag):
+            acc = psum.tile([P, n], F32, name=name, tag=tag)
             nc.tensor.matmul_mx(acc[:], lhsT=wq[0][:].bitcast(FP8X4), lhsT_scale=wq[1][:],
                                 rhs=words.bitcast(FP8X4), rhs_scale=plane, start=True, stop=True)
             return acc
@@ -83,66 +82,66 @@ def tile_attend_tctwotables_kernel(tc, tab_words, tab_scales, dtab_words, dtab_s
         s2 = load_scales("s2", tab2_scales, sy, ve)
         list1 = load_list("list1", offs)
         s1 = load_scales("s1", tab_scales, sy, ve)
-        sd2 = load_scales("sd2", dtab2_scales, sy, ve)
+        sd2 = load_scales("sd2", dtab2_scales, sy, gp)
+        sd1 = load_scales("sd1", dtab_scales, sy, gp)
         x2 = load_words("x2", tab2_words, sy, "A")
         w2_raw = load_weight("w2_raw", w2, sy, "B")
         x1 = load_words("x1", tab_words, sy, "C")
-        sd1 = load_scales("sd1", dtab_scales, sy, ve)
+        w1_raw = load_weight("w1_raw", w1, sy, "D")
         bias_c = keep.tile([P, 1], F32, name="bias_c")
         og_c = keep.tile([P, 1], F32, name="og_c")
         ac.dma_start(bias_c[:], bias)
-        ac.dma_start(og_c[:], og)
+        sy.dma_start(og_c[:], og)
+        warm = keep.tile([P, 1], F32, name="warm")
+        nc.scalar.activation(warm[:], bias_c[:], ACT.Sigmoid)
 
         rows = keep.tile([P, 2 * J], U8, name="rows")
         gather_rows(rows, 0, s2, list2)
         gather_rows(rows, 1, s1, list1)
         plane = spread_rows("plane", rows, sy)
-        w1_raw = load_weight("w1_raw", w1, sy, "s1")
+        xd2 = load_words("xd2", dtab2_words, sy, "s1")
         drows = keep.tile([P, 2 * J], U8, name="drows")
         gather_rows(drows, 0, sd2, list2)
-        xd2 = load_words("xd2", dtab2_words, sy, "sd2")
+        gather_rows(drows, 1, sd1, list1)
+        dplane = spread_rows("dplane", drows, sy)
+        xd1 = load_words("xd1", dtab_words, sy, "sd1")
 
         gx2 = gather("gx2", x2, list2[:], U32, J)
         w2q = quantise("w2", w2_raw)
-        xd1 = load_words("xd1", dtab_words, sy, "A")
         base_sb = keep.tile([P, J], F32, name="base_sb", tag="B")
         sy.dma_start(base_sb[:], base)
-        b = product("b", w2q, gx2[:], plane[:, 0:J], J)
-        half_bias = keep.tile([P, 1], F32, name="half_bias")
-        nc.scalar.mul(half_bias[:], bias_c[:], 0.5)
-        tau = keep.tile([P, J], F32, name="tau")
-        nc.scalar.activation(tau[:], b[:], ACT.Tanh, bias=half_bias[:], scale=0.5)
+        b = product("b", w2q, gx2[:], plane[:, 0:J], J, "fwd")
+        g = keep.tile([P, J], F32, name="g")
+        nc.scalar.activation(g[:], b[:], ACT.Sigmoid, bias=bias_c[:])
         gq = keep.tile([P, J], F32, name="gq")
-        nc.scalar.activation(gq[:], tau[:], ACT.Square, scale=0.5)
+        nc.scalar.activation(gq[:], g[:], ACT.Square, bias=-0.5)
 
         gx1 = gather("gx1", x1, list1[:], U32, J)
         w1q = quantise("w1", w1_raw)
-        gather_rows(drows, 1, sd1, list1)
-        dplane = spread_rows("dplane", drows, sy)
-        a = product("a", w1q, gx1[:], plane[:, J:2 * J], J)
+        a = product("a", w1q, gx1[:], plane[:, J:2 * J], J, "fwd")
         h = keep.tile([P, J], F32, name="h")
         nc.scalar.activation(h[:], a[:], ACT.Tanh)
         hq = keep.tile([P, J], F32, name="hq")
         nc.scalar.activation(hq[:], h[:], ACT.Square)
-        g = keep.tile([P, J], F32, name="g")
-        nc.scalar.activation(g[:], tau[:], ACT.Identity, bias=0.5, scale=0.5)
 
         gxd2 = gather("gxd2", xd2, list2[:], U32, J)
-        tb = product("tb", w2q, gxd2[:], dplane[:, 0:J], J)
+        tb = product("tb", w2q, gxd2[:], dplane[:, 0:J], J, "tb")
 
-        factors = keep.tile([P, 2 * J], F32, name="factors", tag="sd2")
+        factors = keep.tile([P, 2 * J], F32, name="factors", tag="s1")
         fb, fa = factors[:, 0:J], factors[:, J:2 * J]
         nc.vector.scalar_tensor_tensor(fb, gq[:], 0.25, h[:], ALU.subtract, ALU.mult)
         nc.vector.scalar_tensor_tensor(fa, hq[:], 1.0, g[:], ALU.subtract, ALU.mult)
         tb_term = keep.tile([P, J], F32, name="tb_term")
         nc.vector.scalar_tensor_tensor(tb_term[:], tb[:], og_c[:], fb, ALU.mult, ALU.mult)
         part = keep.tile([P, J], F32, name="part")
-        nc.vector.tensor_tensor(part[:], base_sb[:], tb_term[:], ALU.subtract)
+        for i in range(2):
+            cols = slice(i * HALF, (i + 1) * HALF)
+            nc.gpsimd.tensor_tensor(part[:, cols], base_sb[:, cols], tb_term[:, cols], ALU.subtract)
 
         halves = []
         for i in range(2):
             gx = gather("gxd1_%d" % i, xd1, list1[:, i * 16:(i + 1) * 16], U32, HALF)
-            halves.append(product("ta%d" % i, w1q, gx[:], dplane[:, J + i * HALF:J + (i + 1) * HALF], HALF))
+            halves.append(product("ta%d" % i, w1q, gx[:], dplane[:, J + i * HALF:J + (i + 1) * HALF], HALF, "ta%d" % i))
         for i in range(2):
             cols = slice(i * HALF, (i + 1) * HALF)
             ta_term = keep.tile([P, HALF], F32, name="ta_term%d" % i)

@@ -15,8 +15,14 @@ ACT = mybir.ActivationFunctionType
 P = 128
 K, R, T, J = 512, 128, 2048, 512
 FLOPS = 4 * 2 * K * R * J
+PACK = 4
+SCALE_ROWS = K // 32
+QUADRANTS = 4
 HALF = J // 2
-ROW0 = P - 16
+HALF_COLUMNS = HALF // 16
+
+VALUE_ROW0, VALUE_FIRST = 112, 0
+TANGENT_ROW0, TANGENT_FIRST = 48, 4
 
 
 def tile_attend_tctwotables_kernel(tc, tab_words, tab_scales, dtab_words, dtab_scales, w1,
@@ -28,124 +34,133 @@ def tile_attend_tctwotables_kernel(tc, tab_words, tab_scales, dtab_words, dtab_s
         psum = ctx.enter_context(tc.psum_pool(name="psum", bufs=1))
 
         def load_list(name, src):
-            t = keep.tile([P, J // 16], U16, name=name)
-            nc.sync.dma_start(t[:], src)
-            return t
+            offsets = keep.tile([P, J // 16], U16, name=name)
+            nc.sync.dma_start(offsets[:], src)
+            return offsets
 
-        def load_words(name, src, q, tag):
-            t = keep.tile([P, T], U32, name=name, tag=tag)
-            q.dma_start(t[:].bitcast(I32), src[0].rearrange("p n t -> p (n t)").bitcast(I32))
-            return t
+        def load_words(name, src, tag):
+            window = keep.tile([P, T], U32, name=name, tag=tag)
+            nc.sync.dma_start(window[:].bitcast(I32), src[0].rearrange("p n t -> p (n t)").bitcast(I32))
+            return window
 
-        def load_scales(name, src, q, eng):
-            t = keep.tile([P, T], U8, name=name, tag=name)
-            q.dma_start(t[ROW0:P, :].bitcast(I32), src[0].bitcast(I32))
-            eng.memset(t[0:ROW0, :].bitcast(I32), 0)
-            return t
+        def load_scales(name, src, row0, zeroing_engine):
+            window = keep.tile([P, T], U8, name=name, tag=name)
+            end = row0 + SCALE_ROWS
+            nc.sync.dma_start(window[row0:end, :].bitcast(I32), src[0].bitcast(I32))
+            zeroing_engine.memset(window[0:row0, :].bitcast(I32), 0)
+            if end < P:
+                zeroing_engine.memset(window[end:P, :].bitcast(I32), 0)
+            return window
 
-        def gather_rows(rows, i, window, offsets):
-            nc.vector.tensor_copy(rows[:, i * J:(i + 1) * J], window[:].indirect(offsets[:]))
+        def gather_scales(rows, place, window, offsets):
+            nc.vector.tensor_copy(rows[:, place * J:(place + 1) * J], window[:].indirect(offsets[:]))
 
-        def spread_rows(name, rows, q):
+        def spread_scales(name, rows, row0, first):
             plane = keep.tile([P, 2 * J], U8, name=name, align_bytes=64)
-            for quad in range(4):
-                q.dma_start(plane[32 * quad: 32 * quad + 4, :].bitcast(I32),
-                            rows[ROW0 + 4 * quad: ROW0 + 4 * quad + 4, :].bitcast(I32))
+            for quad in range(QUADRANTS):
+                nc.sync.dma_start(plane[32 * quad + first:32 * quad + first + 4, :].bitcast(I32),
+                                  rows[row0 + 4 * quad:row0 + 4 * quad + 4, :].bitcast(I32))
             return plane
 
-        def load_weight(name, src, q, tag):
-            t = keep.tile([P, 4, R], F32, name=name, tag=tag)
-            q.dma_start(t[:], src.rearrange("(p j) r -> p j r", j=4))
-            return t
+        def load_weight(name, src):
+            raw = keep.tile([P, PACK, R], F32, name=name, tag=name)
+            nc.sync.dma_start(raw[:], src.rearrange("(p t) r -> p t r", t=PACK))
+            return raw
 
         def quantise(name, raw):
-            woven = keep.tile([P, R, 4], BF16, name=name + "_bf", align_bytes=64)
-            nc.scalar.copy(woven[:], raw[:].rearrange("p j r -> p r j"))
+            woven = keep.tile([P, R, PACK], BF16, name=name + "_bf16", align_bytes=64)
+            nc.scalar.copy(woven[:], raw[:].rearrange("p t r -> p r t"))
             codes = keep.tile([P, R], U32, name=name + "_codes", align_bytes=64)
             scales = keep.tile([P, R], U8, name=name + "_scales", align_bytes=64)
-            nc.vector.quantize_mx(codes[:].bitcast(FP8X4), scales[:], woven[:].rearrange("p r j -> p (r j)"))
+            nc.vector.quantize_mx(codes[:].bitcast(FP8X4), scales[:], woven[:].rearrange("p r t -> p (r t)"))
             return codes, scales
 
-        def gather(name, window, offsets, dtype, n):
-            g = keep.tile([P, n], dtype, name=name, align_bytes=64)
-            nc.vector.tensor_copy(g[:], window[:].indirect(offsets))
-            return g
+        def gather_words(name, window, offsets, count):
+            words = keep.tile([P, count], U32, name=name, align_bytes=64)
+            nc.vector.tensor_copy(words[:], window[:].indirect(offsets))
+            return words
 
-        def product(name, wq, words, plane, n, tag):
-            acc = psum.tile([P, n], F32, name=name, tag=tag)
-            nc.tensor.matmul_mx(acc[:], lhsT=wq[0][:].bitcast(FP8X4), lhsT_scale=wq[1][:],
-                                rhs=words.bitcast(FP8X4), rhs_scale=plane, start=True, stop=True)
+        def product(name, weight, words, plane, count):
+            codes, scales = weight
+            acc = psum.tile([P, count], F32, name=name)
+            nc.tensor.matmul_mx(acc[:], lhsT=codes[:].bitcast(FP8X4), lhsT_scale=scales[:],
+                                rhs=words[:].bitcast(FP8X4), rhs_scale=plane, start=True, stop=True)
             return acc
 
-        sy, ac, gp, ve = nc.sync, nc.scalar, nc.gpsimd, nc.vector
         list2 = load_list("list2", offs2)
-        s2 = load_scales("s2", tab2_scales, sy, ve)
+        tab2_sw = load_scales("tab2_sw", tab2_scales, VALUE_ROW0, nc.vector)
         list1 = load_list("list1", offs)
-        s1 = load_scales("s1", tab_scales, sy, ve)
-        sd2 = load_scales("sd2", dtab2_scales, sy, gp)
-        sd1 = load_scales("sd1", dtab_scales, sy, gp)
-        x2 = load_words("x2", tab2_words, sy, "A")
-        w2_raw = load_weight("w2_raw", w2, sy, "B")
-        x1 = load_words("x1", tab_words, sy, "C")
-        w1_raw = load_weight("w1_raw", w1, sy, "D")
-        bias_c = keep.tile([P, 1], F32, name="bias_c")
-        og_c = keep.tile([P, 1], F32, name="og_c")
-        ac.dma_start(bias_c[:], bias)
-        sy.dma_start(og_c[:], og)
-        warm = keep.tile([P, 1], F32, name="warm")
-        nc.scalar.activation(warm[:], bias_c[:], ACT.Sigmoid)
+        tab_sw = load_scales("tab_sw", tab_scales, VALUE_ROW0, nc.vector)
+        dtab2_sw = load_scales("dtab2_sw", dtab2_scales, TANGENT_ROW0, nc.gpsimd)
+        dtab_sw = load_scales("dtab_sw", dtab_scales, TANGENT_ROW0, nc.gpsimd)
+        tab2_ww = load_words("tab2_ww", tab2_words, "tab2_ww")
+        w2_raw = load_weight("w2_raw", w2)
+        tab_ww = load_words("tab_ww", tab_words, "tab_ww")
+        w1_raw = load_weight("w1_raw", w1)
+        bias_col = keep.tile([P, 1], F32, name="bias_col")
+        og_col = keep.tile([P, 1], F32, name="og_col")
+        nc.scalar.dma_start(bias_col[:], bias)
+        nc.sync.dma_start(og_col[:], og)
+        warm_up = keep.tile([P, 1], F32, name="warm_up")
+        nc.scalar.activation(warm_up[:], bias_col[:], ACT.Sigmoid)
 
-        rows = keep.tile([P, 2 * J], U8, name="rows")
-        gather_rows(rows, 0, s2, list2)
-        gather_rows(rows, 1, s1, list1)
-        plane = spread_rows("plane", rows, sy)
-        xd2 = load_words("xd2", dtab2_words, sy, "s1")
-        drows = keep.tile([P, 2 * J], U8, name="drows")
-        gather_rows(drows, 0, sd2, list2)
-        gather_rows(drows, 1, sd1, list1)
-        dplane = spread_rows("dplane", drows, sy)
-        xd1 = load_words("xd1", dtab_words, sy, "sd1")
+        value_rows = keep.tile([P, 2 * J], U8, name="value_rows")
+        gather_scales(value_rows, 0, tab2_sw, list2)
+        gather_scales(value_rows, 1, tab_sw, list1)
+        value_plane = spread_scales("value_plane", value_rows, VALUE_ROW0, VALUE_FIRST)
+        dtab2_ww = load_words("dtab2_ww", dtab2_words, "tab_sw")
+        tangent_rows = keep.tile([P, 2 * J], U8, name="tangent_rows")
+        gather_scales(tangent_rows, 0, dtab2_sw, list2)
+        gather_scales(tangent_rows, 1, dtab_sw, list1)
+        tangent_plane = spread_scales("tangent_plane", tangent_rows, TANGENT_ROW0, TANGENT_FIRST)
+        dtab_ww = load_words("dtab_ww", dtab_words, "dtab_sw")
 
-        gx2 = gather("gx2", x2, list2[:], U32, J)
-        w2q = quantise("w2", w2_raw)
-        base_sb = keep.tile([P, J], F32, name="base_sb", tag="B")
-        sy.dma_start(base_sb[:], base)
-        b = product("b", w2q, gx2[:], plane[:, 0:J], J, "fwd")
+        tab2_words_g = gather_words("tab2_words_g", tab2_ww, list2[:], J)
+        w2_mx = quantise("w2", w2_raw)
+        base_sb = keep.tile([P, J], F32, name="base_sb", tag="w2_raw")
+        nc.sync.dma_start(base_sb[:], base)
+        b = product("b", w2_mx, tab2_words_g, value_plane[VALUE_FIRST:P, 0:J], J)
         g = keep.tile([P, J], F32, name="g")
-        nc.scalar.activation(g[:], b[:], ACT.Sigmoid, bias=bias_c[:])
-        gq = keep.tile([P, J], F32, name="gq")
-        nc.scalar.activation(gq[:], g[:], ACT.Square, bias=-0.5)
+        nc.scalar.activation(g[:], b[:], ACT.Sigmoid, bias=bias_col[:])
+        g_centred_sq = keep.tile([P, J], F32, name="g_centred_sq")
+        nc.scalar.activation(g_centred_sq[:], g[:], ACT.Square, bias=-0.5)
 
-        gx1 = gather("gx1", x1, list1[:], U32, J)
-        w1q = quantise("w1", w1_raw)
-        a = product("a", w1q, gx1[:], plane[:, J:2 * J], J, "fwd")
+        w1_mx = quantise("w1", w1_raw)
         h = keep.tile([P, J], F32, name="h")
-        nc.scalar.activation(h[:], a[:], ACT.Tanh)
-        hq = keep.tile([P, J], F32, name="hq")
-        nc.scalar.activation(hq[:], h[:], ACT.Square)
+        for i in range(2):
+            words = gather_words("tab_words_g%d" % i, tab_ww,
+                                 list1[:, i * HALF_COLUMNS:(i + 1) * HALF_COLUMNS], HALF)
+            a = product("a%d" % i, w1_mx, words,
+                        value_plane[VALUE_FIRST:P, J + i * HALF:J + (i + 1) * HALF], HALF)
+            nc.scalar.activation(h[:, i * HALF:(i + 1) * HALF], a[:], ACT.Tanh)
+        h_sq = keep.tile([P, J], F32, name="h_sq")
+        nc.scalar.activation(h_sq[:], h[:], ACT.Square)
 
-        gxd2 = gather("gxd2", xd2, list2[:], U32, J)
-        tb = product("tb", w2q, gxd2[:], dplane[:, 0:J], J, "tb")
+        dtab2_words_g = gather_words("dtab2_words_g", dtab2_ww, list2[:], J)
+        tb = product("tb", w2_mx, dtab2_words_g, tangent_plane[TANGENT_FIRST:P, 0:J], J)
 
-        factors = keep.tile([P, 2 * J], F32, name="factors", tag="s1")
-        fb, fa = factors[:, 0:J], factors[:, J:2 * J]
-        nc.vector.scalar_tensor_tensor(fb, gq[:], 0.25, h[:], ALU.subtract, ALU.mult)
-        nc.vector.scalar_tensor_tensor(fa, hq[:], 1.0, g[:], ALU.subtract, ALU.mult)
-        tb_term = keep.tile([P, J], F32, name="tb_term")
-        nc.vector.scalar_tensor_tensor(tb_term[:], tb[:], og_c[:], fb, ALU.mult, ALU.mult)
-        part = keep.tile([P, J], F32, name="part")
+        factors = keep.tile([P, 2 * J], F32, name="factors", tag="tab_sw")
+        neg_factor_tb, neg_factor_ta = factors[:, 0:J], factors[:, J:2 * J]
+        nc.vector.scalar_tensor_tensor(neg_factor_tb, g_centred_sq[:], 0.25, h[:], ALU.subtract, ALU.mult)
+        nc.vector.scalar_tensor_tensor(neg_factor_ta, h_sq[:], 1.0, g[:], ALU.subtract, ALU.mult)
+        neg_term_tb = keep.tile([P, J], F32, name="neg_term_tb")
+        nc.vector.scalar_tensor_tensor(neg_term_tb[:], tb[:], og_col[:], neg_factor_tb, ALU.mult, ALU.mult)
+        partial = keep.tile([P, J], F32, name="partial")
         for i in range(2):
             cols = slice(i * HALF, (i + 1) * HALF)
-            nc.gpsimd.tensor_tensor(part[:, cols], base_sb[:, cols], tb_term[:, cols], ALU.subtract)
+            nc.gpsimd.tensor_tensor(partial[:, cols], base_sb[:, cols], neg_term_tb[:, cols], ALU.subtract)
 
-        halves = []
+        ta_halves = []
         for i in range(2):
-            gx = gather("gxd1_%d" % i, xd1, list1[:, i * 16:(i + 1) * 16], U32, HALF)
-            halves.append(product("ta%d" % i, w1q, gx[:], dplane[:, J + i * HALF:J + (i + 1) * HALF], HALF, "ta%d" % i))
+            words = gather_words("dtab_words_g%d" % i, dtab_ww,
+                                 list1[:, i * HALF_COLUMNS:(i + 1) * HALF_COLUMNS], HALF)
+            ta_halves.append(product("ta%d" % i, w1_mx, words,
+                                     tangent_plane[TANGENT_FIRST:P, J + i * HALF:J + (i + 1) * HALF], HALF))
         for i in range(2):
             cols = slice(i * HALF, (i + 1) * HALF)
-            ta_term = keep.tile([P, HALF], F32, name="ta_term%d" % i)
-            nc.vector.scalar_tensor_tensor(ta_term[:], halves[i][:], og_c[:], factors[:, J + i * HALF:J + (i + 1) * HALF], ALU.mult, ALU.mult)
-            res = keep.tile([P, HALF], F32, name="res%d" % i)
-            nc.vector.tensor_tensor(res[:], part[:, cols], ta_term[:], ALU.subtract)
-            nc.sync.dma_start(out[:, cols], res[:])
+            neg_term_ta = keep.tile([P, HALF], F32, name="neg_term_ta%d" % i)
+            nc.vector.scalar_tensor_tensor(neg_term_ta[:], ta_halves[i][:], og_col[:],
+                                           factors[:, J + i * HALF:J + (i + 1) * HALF], ALU.mult, ALU.mult)
+            result = keep.tile([P, HALF], F32, name="result%d" % i)
+            nc.vector.tensor_tensor(result[:], partial[:, cols], neg_term_ta[:], ALU.subtract)
+            nc.sync.dma_start(out[:, cols], result[:])

from contextlib import ExitStack

import concourse.mybir as mybir

F32 = mybir.dt.float32
BF16 = mybir.dt.bfloat16
I32 = mybir.dt.int32
U32 = mybir.dt.uint32
U16 = mybir.dt.uint16
U8 = mybir.dt.uint8
FP8X4 = mybir.dt.float8_e4m3fn_x4
ALU = mybir.AluOpType
ACT = mybir.ActivationFunctionType

P = 128
K, R, T, J = 512, 128, 2048, 512
FLOPS = 4 * 2 * K * R * J
PACK = 4
SCALE_ROWS = K // 32
QUADRANTS = 4
HALF = J // 2
HALF_COLUMNS = HALF // 16

VALUE_ROW0, VALUE_FIRST = 112, 0
TANGENT_ROW0, TANGENT_FIRST = 48, 4


def tile_attend_tctwotables_kernel(tc, tab_words, tab_scales, dtab_words, dtab_scales, w1,
                                    tab2_words, tab2_scales, dtab2_words, dtab2_scales, w2,
                                    bias, og, base, offs, offs2, out):
    nc = tc.nc
    with ExitStack() as ctx:
        keep = ctx.enter_context(tc.tile_pool(name="keep", bufs=1))
        psum = ctx.enter_context(tc.psum_pool(name="psum", bufs=1))

        def load_list(name, src):
            offsets = keep.tile([P, J // 16], U16, name=name)
            nc.sync.dma_start(offsets[:], src)
            return offsets

        def load_words(name, src, tag):
            window = keep.tile([P, T], U32, name=name, tag=tag)
            nc.sync.dma_start(window[:].bitcast(I32), src[0].rearrange("p n t -> p (n t)").bitcast(I32))
            return window

        def load_scales(name, src, row0, zeroing_engine):
            window = keep.tile([P, T], U8, name=name, tag=name)
            end = row0 + SCALE_ROWS
            nc.sync.dma_start(window[row0:end, :].bitcast(I32), src[0].bitcast(I32))
            zeroing_engine.memset(window[0:row0, :].bitcast(I32), 0)
            if end < P:
                zeroing_engine.memset(window[end:P, :].bitcast(I32), 0)
            return window

        def gather_scales(rows, place, window, offsets):
            nc.vector.tensor_copy(rows[:, place * J:(place + 1) * J], window[:].indirect(offsets[:]))

        def spread_scales(name, rows, row0, first):
            plane = keep.tile([P, 2 * J], U8, name=name, align_bytes=64)
            for quad in range(QUADRANTS):
                nc.sync.dma_start(plane[32 * quad + first:32 * quad + first + 4, :].bitcast(I32),
                                  rows[row0 + 4 * quad:row0 + 4 * quad + 4, :].bitcast(I32))
            return plane

        def load_weight(name, src):
            raw = keep.tile([P, PACK, R], F32, name=name, tag=name)
            nc.sync.dma_start(raw[:], src.rearrange("(p t) r -> p t r", t=PACK))
            return raw

        def quantise(name, raw):
            woven = keep.tile([P, R, PACK], BF16, name=name + "_bf16", align_bytes=64)
            nc.scalar.copy(woven[:], raw[:].rearrange("p t r -> p r t"))
            codes = keep.tile([P, R], U32, name=name + "_codes", align_bytes=64)
            scales = keep.tile([P, R], U8, name=name + "_scales", align_bytes=64)
            nc.vector.quantize_mx(codes[:].bitcast(FP8X4), scales[:], woven[:].rearrange("p r t -> p (r t)"))
            return codes, scales

        def gather_words(name, window, offsets, count):
            words = keep.tile([P, count], U32, name=name, align_bytes=64)
            nc.vector.tensor_copy(words[:], window[:].indirect(offsets))
            return words

        def product(name, weight, words, plane, count):
            codes, scales = weight
            acc = psum.tile([P, count], F32, name=name)
            nc.tensor.matmul_mx(acc[:], lhsT=codes[:].bitcast(FP8X4), lhsT_scale=scales[:],
                                rhs=words[:].bitcast(FP8X4), rhs_scale=plane, start=True, stop=True)
            return acc

        list2 = load_list("list2", offs2)
        tab2_sw = load_scales("tab2_sw", tab2_scales, VALUE_ROW0, nc.vector)
        list1 = load_list("list1", offs)
        tab_sw = load_scales("tab_sw", tab_scales, VALUE_ROW0, nc.vector)
        dtab2_sw = load_scales("dtab2_sw", dtab2_scales, TANGENT_ROW0, nc.gpsimd)
        dtab_sw = load_scales("dtab_sw", dtab_scales, TANGENT_ROW0, nc.gpsimd)
        tab2_ww = load_words("tab2_ww", tab2_words, "tab2_ww")
        w2_raw = load_weight("w2_raw", w2)
        tab_ww = load_words("tab_ww", tab_words, "tab_ww")
        w1_raw = load_weight("w1_raw", w1)
        bias_col = keep.tile([P, 1], F32, name="bias_col")
        og_col = keep.tile([P, 1], F32, name="og_col")
        nc.scalar.dma_start(bias_col[:], bias)
        nc.sync.dma_start(og_col[:], og)
        warm_up = keep.tile([P, 1], F32, name="warm_up")
        nc.scalar.activation(warm_up[:], bias_col[:], ACT.Sigmoid)

        value_rows = keep.tile([P, 2 * J], U8, name="value_rows")
        gather_scales(value_rows, 0, tab2_sw, list2)
        gather_scales(value_rows, 1, tab_sw, list1)
        value_plane = spread_scales("value_plane", value_rows, VALUE_ROW0, VALUE_FIRST)
        dtab2_ww = load_words("dtab2_ww", dtab2_words, "tab_sw")
        tangent_rows = keep.tile([P, 2 * J], U8, name="tangent_rows")
        gather_scales(tangent_rows, 0, dtab2_sw, list2)
        gather_scales(tangent_rows, 1, dtab_sw, list1)
        tangent_plane = spread_scales("tangent_plane", tangent_rows, TANGENT_ROW0, TANGENT_FIRST)
        dtab_ww = load_words("dtab_ww", dtab_words, "dtab_sw")

        tab2_words_g = gather_words("tab2_words_g", tab2_ww, list2[:], J)
        w2_mx = quantise("w2", w2_raw)
        base_sb = keep.tile([P, J], F32, name="base_sb", tag="w2_raw")
        nc.sync.dma_start(base_sb[:], base)
        b = product("b", w2_mx, tab2_words_g, value_plane[VALUE_FIRST:P, 0:J], J)
        g = keep.tile([P, J], F32, name="g")
        nc.scalar.activation(g[:], b[:], ACT.Sigmoid, bias=bias_col[:])
        g_centred_sq = keep.tile([P, J], F32, name="g_centred_sq")
        nc.scalar.activation(g_centred_sq[:], g[:], ACT.Square, bias=-0.5)

        w1_mx = quantise("w1", w1_raw)
        h = keep.tile([P, J], F32, name="h")
        for i in range(2):
            words = gather_words("tab_words_g%d" % i, tab_ww,
                                 list1[:, i * HALF_COLUMNS:(i + 1) * HALF_COLUMNS], HALF)
            a = product("a%d" % i, w1_mx, words,
                        value_plane[VALUE_FIRST:P, J + i * HALF:J + (i + 1) * HALF], HALF)
            nc.scalar.activation(h[:, i * HALF:(i + 1) * HALF], a[:], ACT.Tanh)
        h_sq = keep.tile([P, J], F32, name="h_sq")
        nc.scalar.activation(h_sq[:], h[:], ACT.Square)

        dtab2_words_g = gather_words("dtab2_words_g", dtab2_ww, list2[:], J)
        tb = product("tb", w2_mx, dtab2_words_g, tangent_plane[TANGENT_FIRST:P, 0:J], J)

        factors = keep.tile([P, 2 * J], F32, name="factors", tag="tab_sw")
        neg_factor_tb, neg_factor_ta = factors[:, 0:J], factors[:, J:2 * J]
        nc.vector.scalar_tensor_tensor(neg_factor_tb, g_centred_sq[:], 0.25, h[:], ALU.subtract, ALU.mult)
        nc.vector.scalar_tensor_tensor(neg_factor_ta, h_sq[:], 1.0, g[:], ALU.subtract, ALU.mult)
        neg_term_tb = keep.tile([P, J], F32, name="neg_term_tb")
        nc.vector.scalar_tensor_tensor(neg_term_tb[:], tb[:], og_col[:], neg_factor_tb, ALU.mult, ALU.mult)
        partial = keep.tile([P, J], F32, name="partial")
        for i in range(2):
            cols = slice(i * HALF, (i + 1) * HALF)
            nc.gpsimd.tensor_tensor(partial[:, cols], base_sb[:, cols], neg_term_tb[:, cols], ALU.subtract)

        ta_halves = []
        for i in range(2):
            words = gather_words("dtab_words_g%d" % i, dtab_ww,
                                 list1[:, i * HALF_COLUMNS:(i + 1) * HALF_COLUMNS], HALF)
            ta_halves.append(product("ta%d" % i, w1_mx, words,
                                     tangent_plane[TANGENT_FIRST:P, J + i * HALF:J + (i + 1) * HALF], HALF))
        for i in range(2):
            cols = slice(i * HALF, (i + 1) * HALF)
            neg_term_ta = keep.tile([P, HALF], F32, name="neg_term_ta%d" % i)
            nc.vector.scalar_tensor_tensor(neg_term_ta[:], ta_halves[i][:], og_col[:],
                                           factors[:, J + i * HALF:J + (i + 1) * HALF], ALU.mult, ALU.mult)
            result = keep.tile([P, HALF], F32, name="result%d" % i)
            nc.vector.tensor_tensor(result[:], partial[:, cols], neg_term_ta[:], ALU.subtract)
            nc.sync.dma_start(out[:, cols], result[:])
